import numpy as np
import ml_dtypes


def mxq(x, axis, fmt="e4m3"):
    dtype, down = {"e4m3": (ml_dtypes.float8_e4m3fn, 7), "e5m2": (ml_dtypes.float8_e5m2, 14)}[fmt]
    v = np.moveaxis(np.asarray(x, np.float32).astype(ml_dtypes.bfloat16).astype(np.float64), axis, -1)
    blocks = v.reshape(v.shape[:-1] + (-1, 32))
    amax = np.abs(blocks).max(-1, keepdims=True)
    byte = np.maximum(np.where(amax > 0, np.frexp(amax)[1] - 1 + 127, 0) - down, 1)
    scale = np.exp2(byte - 127.0)
    codes = (blocks / scale).astype(np.float32).astype(dtype).astype(np.float64)
    return np.moveaxis((codes * scale).reshape(v.shape), -1, axis)


WIDE = False


def mx_kscale(k):
    if not WIDE:
        return np.ones(k)
    levels = np.array([30, -30])
    if k % 512:
        return np.exp2(np.random.permutation(np.resize(levels, k // 32))).repeat(32)
    a = np.empty((k // 512, 16))
    for p in range(k // 512):
        a[p, :8] = np.random.permutation(np.resize(levels, 8))
        for g in range(8):
            far = levels[np.abs(levels - a[p, g]) >= 10]
            a[p, g + 8] = far[np.random.randint(len(far))]
    return np.exp2(a.ravel()).repeat(32)


def f64(x):
    return np.asarray(x).astype(np.float64)


def striped(idx):
    return np.tile(np.asarray(idx).reshape(-1, 16).T, (8, 1)).astype(np.uint16)


def unstriped(offs):
    return offs[:16].T.reshape(-1).astype(np.int64)


E2M1 = np.array([0.0, 0.5, 1.0, 1.5, 2.0, 3.0, 4.0, 6.0, -0.0, -0.5, -1.0, -1.5, -2.0, -3.0, -4.0, -6.0])


def pack_weight(w, fmt):
    k, n = w.shape
    w = f64(np.asarray(w, np.float32).astype(ml_dtypes.bfloat16)).reshape(k // 32, 32, n)
    amax = np.abs(w).max(1)
    if fmt in ("e4m3", "e5m2"):
        byte = np.frexp(amax)[1] - 1 + 127 - (7 if fmt == "e4m3" else 14)
    else:
        mant, ex = np.frexp(amax / 6.0)
        byte = np.where(mant > 0.5, ex, ex - 1) + 127
    byte = np.clip(np.where(amax > 0, byte, 1), 1, 254)
    scaled = (w * np.exp2(127.0 - byte)[:, None, :]).reshape(k, n).astype(np.float32)
    by_word = np.ascontiguousarray(scaled.reshape(k // 512, 128, 4, n).transpose(0, 1, 3, 2))
    if fmt in ("e4m3", "e5m2"):
        words = by_word.astype(ml_dtypes.float8_e4m3fn if fmt == "e4m3" else ml_dtypes.float8_e5m2).view(np.uint8)
    else:
        c = by_word.astype(ml_dtypes.float4_e2m1fn).view(np.uint8) & 0xF
        words = (c[..., 0::2] | (c[..., 1::2] << 4)).reshape(k // 512, 128, 2 * n)
    return np.ascontiguousarray(words), np.ascontiguousarray(byte.astype(np.uint8).reshape(k // 512, 16, n))


def unpack_weight(words, scales, fmt):
    g, _, n = scales.shape
    words = np.ascontiguousarray(words).reshape(g, 128, n, -1)
    if fmt in ("e4m3", "e5m2"):
        vals = words.view(ml_dtypes.float8_e4m3fn if fmt == "e4m3" else ml_dtypes.float8_e5m2).astype(np.float64)
    else:
        nib = np.empty((g, 128, n, 4), np.uint8)
        nib[..., 0::2] = words & 0xF
        nib[..., 1::2] = words >> 4
        vals = E2M1[nib]
    vals = vals * np.repeat(np.exp2(scales.astype(np.float64) - 127.0), 8, axis=1)[..., None]
    return vals.transpose(0, 1, 3, 2).reshape(g * 512, n)


K, T, J, R, N, S = 512, 1024, 256, 512, 256, 1024


def setup_inputs():
    n = np.random.standard_normal
    idx = np.random.permutation(T)[:J]
    idx2 = np.random.permutation(T)[:J]
    idx3 = np.random.permutation(J)[:J]
    idx4 = np.random.permutation(S)[:N]
    fk = mx_kscale(K)
    fr = mx_kscale(R)
    wp = pack_weight(n((K, R)) * 1 / np.sqrt(K) / fk[:, None] * fr, "e2m1")
    vsp = pack_weight(n((R, S)) * 1 / np.sqrt(R) / fr[:, None], "e5m2")
    return {
        "cq": (np.random.randint(-7, 8, (K, T)).astype(np.float64)).astype(np.float32),
        "ga": (np.random.uniform(0.1, 0.4, (K, 1)) * fk[:, None]).astype(np.float32),
        "gb": (np.random.uniform(0.1, 0.4, (K, 1)) * fk[:, None]).astype(np.float32),
        "w_words": wp[0],
        "w_scales": wp[1],
        "sa": (np.random.uniform(0.5, 1.6, (R, 1))).astype(np.float32),
        "vs_words": vsp[0],
        "vs_scales": vsp[1],
        "offs": striped(idx),
        "offs2": striped(idx2),
        "offs3": striped(idx3),
        "offs4": striped(idx4),
    }


def reference(cq, ga, gb, w_words, w_scales, sa, vs_words, vs_scales, offs, offs2, offs3, offs4):
    idx = unstriped(offs)
    idx2 = unstriped(offs2)
    idx3 = unstriped(offs3)
    idx4 = unstriped(offs4)
    wu = unpack_weight(w_words, w_scales, "e2m1")
    vsu = unpack_weight(vs_words, vs_scales, "e5m2")
    x1 = f64(cq)[:, idx] * f64(ga)
    x2 = f64(cq)[:, idx2] * f64(gb)
    x1q = mxq(x1, 0, "e4m3")
    a = wu.T @ x1q
    x2q = mxq(x2, 0, "e4m3")
    b = wu.T @ x2q
    hid = np.abs(a - b[:, idx3] * f64(sa))
    vsidx4g = vsu[:, idx4]
    hidq = mxq(hid, 0, "e4m3")
    y = vsidx4g.T @ hidq
    return y

@@ -1,0 +1,205 @@
+from contextlib import ExitStack
+
+import concourse.mybir as mybir
+
+K, T, J, R, N, S = 512, 1024, 256, 512, 256, 1024
+FLOPS = 2 * K * R * J * 2 + 2 * R * N * J
+
+F32 = mybir.dt.float32
+BF16 = mybir.dt.bfloat16
+I32 = mybir.dt.int32
+U32 = mybir.dt.uint32
+U16 = mybir.dt.uint16
+U8 = mybir.dt.uint8
+E4M3 = mybir.dt.float8_e4m3fn_x4
+E5M2 = mybir.dt.float8_e5m2_x4
+E2M1 = mybir.dt.float4_e2m1fn_x4
+ACT = mybir.ActivationFunctionType
+ALU = mybir.AluOpType
+
+P = 128
+PACK = 4
+HALF = J // 2
+LIST_COLS = 16
+
+
+def tile_list_scaledpartner_twosteps_store_plain_kernel(
+    tc, cq, ga, gb, w_words, w_scales, sa, vs_words, vs_scales, offs, offs2, offs3, offs4, out
+):
+    nc = tc.nc
+    with ExitStack() as ctx:
+        lists = ctx.enter_context(tc.tile_pool(name="lists", bufs=1))
+        sb = ctx.enter_context(tc.tile_pool(name="sb", bufs=1))
+        psum = ctx.enter_context(tc.psum_pool(name="psum", bufs=1))
+
+        def tile(name, shape, dtype, tag=None):
+            return sb.tile(shape, dtype, name=name, tag=tag or name, align_bytes=64)
+
+        def list_tile(name):
+            return lists.tile([P, LIST_COLS], U16, name=name)
+
+        idx1, idx2, idx3, idx4 = [list_tile("idx%d" % i) for i in range(1, 5)]
+        cq_rows = cq.rearrange("(p t) c -> p t c", t=PACK)
+        table = [tile("table%d" % t, [P, T], F32) for t in range(PACK)]
+        ga_t, gb_t, sa_t = [tile(n, [P, PACK], F32) for n in ("ga_t", "gb_t", "sa_t")]
+        w_raw = tile("w_raw", [P, R], U16)
+        ws_rows = tile("ws_rows", [PACK, PACK, R // 4], I32)
+        vss_rows = tile("vss_rows", [PACK, PACK, S // 4], I32)
+        vs_table = tile("vs_table", [P, S], I32)
+
+        def by_partition(v):
+            return v.rearrange("(p t) o -> p (t o)", t=PACK)
+
+        def scale_rows(v):
+            return v[0].bitcast(I32).rearrange("(q r) c -> r q c", r=PACK)
+
+        nc.sync.dma_start(idx2[:], offs2)
+        nc.scalar.dma_start(gb_t[:], by_partition(gb))
+        nc.sync.dma_start(table[0][:], cq_rows[:, 0, :])
+        nc.scalar.dma_start(vss_rows[:], scale_rows(vs_scales))
+        nc.sync.dma_start(idx1[:], offs)
+        nc.scalar.dma_start(ga_t[:], by_partition(ga))
+        nc.sync.dma_start(table[1][:], cq_rows[:, 1, :])
+        nc.scalar.dma_start(ws_rows[:], scale_rows(w_scales))
+        nc.sync.dma_start(w_raw[:].bitcast(I32), w_words[0].bitcast(I32))
+        nc.sync.dma_start(table[2][:], cq_rows[:, 2, :])
+        nc.sync.dma_start(idx4[:], offs4)
+        nc.sync.dma_start(table[3][:], cq_rows[:, 3, :])
+        nc.sync.dma_start(idx3[:], offs3)
+        nc.sync.dma_start(sa_t[:], by_partition(sa))
+        nc.sync.dma_start(vs_table[:], vs_words[0].rearrange("p n t -> p (n t)").bitcast(I32))
+
+
+        def spread(name, rows, width):
+            plane = tile(name, [P, width], U8)
+            nc.vector.memset(plane[:].bitcast(I32), 0)
+            for q in range(PACK):
+                nc.vector.tensor_copy(plane[32 * q : 32 * q + PACK, :].bitcast(I32), rows[:, q, :])
+            return plane
+
+        vss_plane = spread("vss_plane", vss_rows, S)
+        ws_plane = spread("ws_plane", ws_rows, R)
+        w_sc = tile("w_sc", [P, PACK, P], U8)
+        nc.vector.tensor_copy(w_sc[:], ws_plane[:].rearrange("p (m t) -> p t m", t=PACK))
+        w_dealt = tile("w_dealt", [P, PACK, P], U16)
+        nc.vector.tensor_copy(w_dealt[:], w_raw[:].rearrange("p (m t) -> p t m", t=PACK))
+        vs_sc = tile("vs_sc", [P, N], U8)
+        nc.vector.tensor_copy(vs_sc[:], vss_plane[:].indirect(idx4[:]))
+
+        def cols(h):
+            return slice(h * HALF, (h + 1) * HALF)
+
+        n_early = (3, 2)
+        early = [tile("early%d" % i, [P, n_early[i], J], BF16) for i in range(2)]
+        late = [tile("late0", [P, 1, J], BF16), tile("late1", [P, 2, J], BF16)]
+        woven = [[tile("woven%d%d" % (i, h), [P, HALF, PACK], BF16) for h in range(2)] for i in range(2)]
+        x_codes = [tile("x_codes%d" % i, [P, J], U32) for i in range(2)]
+        x_sc = [tile("x_sc%d" % i, [P, J], U8) for i in range(2)]
+        streams = ((idx2, gb_t), (idx1, ga_t))
+
+        for t in range(PACK):
+            for i, (idx, step) in enumerate(streams):
+                dst = early[i][:, t, :] if t < n_early[i] else late[i][:, t - n_early[i], :]
+                nc.scalar.activation(dst, table[t][:].indirect(idx[:]), ACT.Copy, scale=step[:, t : t + 1])
+                if t == n_early[i] - 1:
+                    for h in range(2):
+                        nc.vector.tensor_copy(
+                            woven[i][h][:, :, : n_early[i]], early[i][:, :, cols(h)].rearrange("p t j -> p j t")
+                        )
+
+        for i in range(2):
+            for h in range(2):
+                copy = nc.vector.tensor_copy if i == 0 else nc.scalar.copy
+                copy(woven[i][h][:, :, n_early[i] :], late[i][:, :, cols(h)].rearrange("p t j -> p j t"))
+            for h in range(2):
+                nc.vector.quantize_mx(
+                    out=x_codes[i][:, cols(h)].bitcast(E4M3),
+                    scales=x_sc[i][:, cols(h)],
+                    in_=woven[i][h][:].rearrange("p j t -> p (j t)"),
+                )
+
+
+        def first_stage(dst, t, i, h):
+            nc.tensor.matmul_mx(
+                dst,
+                lhsT=w_dealt[:, t, :].bitcast(E2M1),
+                lhsT_scale=w_sc[:, t, :],
+                rhs=x_codes[i][:, cols(h)].bitcast(E4M3),
+                rhs_scale=x_sc[i][:, cols(h)],
+                start=True,
+                stop=True,
+            )
+
+        b_ps = [psum.tile([P, J], F32, name="b_ps%d" % t, tag="b_ps%d" % t) for t in range(PACK)]
+        b_sb = [tile("b_sb%d" % t, [P, J], F32) for t in range(PACK)]
+        for t in range(PACK):
+            for h in range(2):
+                first_stage(b_ps[t][:, cols(h)], t, 0, h)
+            if t == 0:
+                nc.scalar.copy(b_sb[t][:], b_ps[t][:])
+            else:
+                nc.vector.tensor_copy(b_sb[t][:], b_ps[t][:])
+        a_ps = [psum.tile([P, PACK, HALF], F32, name="a_ps%d" % h) for h in range(2)]
+        for h in range(2):
+            for t in range(PACK):
+                first_stage(a_ps[h][:, t, :], t, 1, h)
+
+        vs_codes = tile("vs_codes", [P, N], U32, tag="woven01")
+        nc.vector.tensor_copy(vs_codes[:], vs_table[:].bitcast(U32).indirect(idx4[:]))
+
+        partner = [tile("partner%d" % h, [P, PACK, HALF], F32) for h in range(2)]
+        diff = [tile("diff%d" % h, [P, PACK, HALF], F32) for h in range(2)]
+        hid = [tile("hid%d" % h, [P, HALF, PACK], BF16) for h in range(2)]
+        hid_codes = [tile("hid_codes%d" % h, [P, HALF], U32) for h in range(2)]
+        hid_sc = [tile("hid_sc%d" % h, [P, HALF], U8) for h in range(2)]
+        for h in range(2):
+            for t in range(PACK):
+                nc.scalar.activation(
+                    partner[h][:, t, :],
+                    b_sb[t][:].indirect(idx3[:, h * 8 : (h + 1) * 8]),
+                    ACT.Copy,
+                    scale=sa_t[:, t : t + 1],
+                )
+                nc.vector.tensor_tensor(diff[h][:, t, :], a_ps[h][:, t, :], partner[h][:, t, :], ALU.subtract)
+            on_vector = HALF if h == 0 else HALF // 2
+            by_slot = diff[h][:, :, :on_vector].rearrange("p t j -> p j t")
+            nc.vector.scalar_tensor_tensor(hid[h][:, :on_vector, :], by_slot, -1.0, by_slot, ALU.mult, ALU.max)
+            if on_vector < HALF:
+                nc.scalar.activation(
+                    hid[h][:, on_vector:, :].rearrange("p (c i) t -> p c t i", i=4),
+                    diff[h][:, :, on_vector:].rearrange("p t (c i) -> p c t i", i=4),
+                    ACT.Abs,
+                )
+        out_rows = out.rearrange("(u p) j -> p u j", p=P)
+        for h in range(2):
+            nc.vector.quantize_mx(out=hid_codes[h][:].bitcast(E4M3), scales=hid_sc[h][:], in_=hid[h][:].rearrange("p j t -> p (j t)"))
+
+            def second_stage(dst, u):
+                nc.tensor.matmul_mx(
+                    dst,
+                    lhsT=vs_codes[:, u * P : (u + 1) * P].bitcast(E5M2),
+                    lhsT_scale=vs_sc[:, u * P : (u + 1) * P],
+                    rhs=hid_codes[h][:].bitcast(E4M3),
+                    rhs_scale=hid_sc[h][:],
+                    start=True,
+                    stop=True,
+                )
+
+            if h == 0:
+                y_ps = psum.tile([P, 2, HALF], F32, name="y_ps0", tag="b_ps0")
+                y_sb = tile("y_sb0", [P, 2, HALF], F32)
+                for u in range(2):
+                    second_stage(y_ps[:, u, :], u)
+                nc.scalar.copy(y_sb[:], y_ps[:])
+                nc.sync.dma_start(out_rows[:, :, cols(h)], y_sb[:])
+            else:
+                for u in range(2):
+                    y_ps = psum.tile([P, HALF], F32, name="y_ps1%d" % u, tag="b_ps%d" % (1 + u))
+                    y_sb = tile("y_sb1%d" % u, [P, HALF], F32)
+                    second_stage(y_ps[:], u)
+                    if u == 0:
+                        nc.vector.tensor_copy(y_sb[:], y_ps[:])
+                        nc.sync.dma_start(out_rows[:, u, cols(h)], y_sb[:])
+                    else:
+                        nc.scalar.copy(y_sb[:], y_ps[:])
+                        nc.scalar.dma_start(out_rows[:, u, cols(h)], y_sb[:])

@@ -69,6 +69,9 @@ def tile_list_scaledpartner_twosteps_store_plain_kernel(
         nc.sync.dma_start(sa_t[:], by_partition(sa))
         nc.sync.dma_start(vs_table[:], vs_words[0].rearrange("p n t -> p (n t)").bitcast(I32))
 
+        warm = tile("warm", [P, 8], F32)
+        nc.vector.memset(warm[:, 0:1], 0.0)
+        nc.scalar.activation(warm[:, 1:2], warm[:, 0:1], ACT.Copy)
 
         def spread(name, rows, width):
             plane = tile(name, [P, width], U8)

@@ -44,7 +44,7 @@ def tile_list_scaledpartner_twosteps_store_plain_kernel(
         ga_t, gb_t, sa_t = [tile(n, [P, PACK], F32) for n in ("ga_t", "gb_t", "sa_t")]
         w_raw = tile("w_raw", [P, R], U16)
         ws_rows = tile("ws_rows", [PACK, PACK, R // 4], I32)
-        vss_rows = tile("vss_rows", [PACK, PACK, S // 4], I32)
+        vss_rows = [tile("vss_rows%d" % g, [P, 2, S // 4], I32) for g in range(2)]
         vs_table = tile("vs_table", [P, S], I32)
 
         def by_partition(v):
@@ -53,14 +53,15 @@ def tile_list_scaledpartner_twosteps_store_plain_kernel(
         def scale_rows(v):
             return v[0].bitcast(I32).rearrange("(q r) c -> r q c", r=PACK)
 
+        nc.sync.dma_start(vss_rows[0][0:PACK, :, :], scale_rows(vs_scales)[:, 0:2, :])
+        nc.scalar.dma_start(vss_rows[1][64 : 64 + PACK, :, :], scale_rows(vs_scales)[:, 2:4, :])
         nc.sync.dma_start(idx2[:], offs2)
-        nc.scalar.dma_start(gb_t[:], by_partition(gb))
         nc.sync.dma_start(table[0][:], cq_rows[:, 0, :])
-        nc.scalar.dma_start(vss_rows[:], scale_rows(vs_scales))
+        nc.scalar.dma_start(gb_t[:], by_partition(gb))
         nc.sync.dma_start(idx1[:], offs)
         nc.scalar.dma_start(ga_t[:], by_partition(ga))
         nc.sync.dma_start(table[1][:], cq_rows[:, 1, :])
-        nc.scalar.dma_start(ws_rows[:], scale_rows(w_scales))
+        nc.sync.dma_start(ws_rows[:], scale_rows(w_scales))
         nc.sync.dma_start(w_raw[:].bitcast(I32), w_words[0].bitcast(I32))
         nc.sync.dma_start(table[2][:], cq_rows[:, 2, :])
         nc.sync.dma_start(idx4[:], offs4)
@@ -77,11 +78,11 @@ def tile_list_scaledpartner_twosteps_store_plain_kernel(
             plane = tile(name, [P, width], U8)
             nc.vector.memset(plane[:].bitcast(I32), 0)
             for q in range(PACK):
-                nc.vector.tensor_copy(plane[32 * q : 32 * q + PACK, :].bitcast(I32), rows[:, q, :])
+                nc.vector.tensor_copy(plane[32 * q : 32 * q + PACK, :].bitcast(I32), rows[q])
             return plane
 
-        vss_plane = spread("vss_plane", vss_rows, S)
-        ws_plane = spread("ws_plane", ws_rows, R)
+        vss_plane = spread("vss_plane", [vss_rows[q // 2][64 * (q // 2) : 64 * (q // 2) + PACK, q % 2, :] for q in range(PACK)], S)
+        ws_plane = spread("ws_plane", [ws_rows[:, q, :] for q in range(PACK)], R)
         w_sc = tile("w_sc", [P, PACK, P], U8)
         nc.vector.tensor_copy(w_sc[:], ws_plane[:].rearrange("p (m t) -> p t m", t=PACK))
         w_dealt = tile("w_dealt", [P, PACK, P], U16)
@@ -150,21 +151,24 @@ def tile_list_scaledpartner_twosteps_store_plain_kernel(
         vs_codes = tile("vs_codes", [P, N], U32, tag="woven01")
         nc.vector.tensor_copy(vs_codes[:], vs_table[:].bitcast(U32).indirect(idx4[:]))
 
-        partner = [tile("partner%d" % h, [P, PACK, HALF], F32) for h in range(2)]
-        diff = [tile("diff%d" % h, [P, PACK, HALF], F32) for h in range(2)]
+        diff = []
         hid = [tile("hid%d" % h, [P, HALF, PACK], BF16) for h in range(2)]
         hid_codes = [tile("hid_codes%d" % h, [P, HALF], U32) for h in range(2)]
         hid_sc = [tile("hid_sc%d" % h, [P, HALF], U8) for h in range(2)]
         for h in range(2):
-            for t in range(PACK):
-                nc.scalar.activation(
-                    partner[h][:, t, :],
-                    b_sb[t][:].indirect(idx3[:, h * 8 : (h + 1) * 8]),
-                    ACT.Copy,
-                    scale=sa_t[:, t : t + 1],
-                )
-                nc.vector.tensor_tensor(diff[h][:, t, :], a_ps[h][:, t, :], partner[h][:, t, :], ALU.subtract)
-            on_vector = HALF if h == 0 else HALF // 2
+            diff.append(tile("diff%d" % h, [P, PACK, HALF], F32, tag="diff"))
+            groups = [(t, t + 1) for t in range(PACK)] if h == 0 else [(0, PACK - 1), (PACK - 1, PACK)]
+            for lo, hi in groups:
+                partner = tile("partner%d%d" % (h, lo), [P, hi - lo, HALF], F32, tag="partner%d" % lo)
+                for t in range(lo, hi):
+                    nc.scalar.activation(
+                        partner[:, t - lo, :],
+                        b_sb[t][:].indirect(idx3[:, h * 8 : (h + 1) * 8]),
+                        ACT.Copy,
+                        scale=sa_t[:, t : t + 1],
+                    )
+                nc.vector.tensor_tensor(diff[h][:, lo:hi, :], a_ps[h][:, lo:hi, :], partner[:], ALU.subtract)
+            on_vector = HALF if h == 0 else 48
             by_slot = diff[h][:, :, :on_vector].rearrange("p t j -> p j t")
             nc.vector.scalar_tensor_tensor(hid[h][:, :on_vector, :], by_slot, -1.0, by_slot, ALU.mult, ALU.max)
             if on_vector < HALF:

@@ -66,9 +66,9 @@ def tile_list_scaledpartner_twosteps_store_plain_kernel(
         nc.sync.dma_start(table[2][:], cq_rows[:, 2, :])
         nc.sync.dma_start(idx4[:], offs4)
         nc.sync.dma_start(table[3][:], cq_rows[:, 3, :])
+        nc.sync.dma_start(vs_table[:], vs_words[0].rearrange("p n t -> p (n t)").bitcast(I32))
         nc.sync.dma_start(idx3[:], offs3)
         nc.sync.dma_start(sa_t[:], by_partition(sa))
-        nc.sync.dma_start(vs_table[:], vs_words[0].rearrange("p n t -> p (n t)").bitcast(I32))
 
         warm = tile("warm", [P, 8], F32)
         nc.vector.memset(warm[:, 0:1], 0.0)
@@ -96,7 +96,8 @@ def tile_list_scaledpartner_twosteps_store_plain_kernel(
         n_early = (3, 2)
         early = [tile("early%d" % i, [P, n_early[i], J], BF16) for i in range(2)]
         late = [tile("late0", [P, 1, J], BF16), tile("late1", [P, 2, J], BF16)]
-        woven = [[tile("woven%d%d" % (i, h), [P, HALF, PACK], BF16) for h in range(2)] for i in range(2)]
+        woven1 = tile("woven1", [P, J, PACK], BF16)
+        woven = [[tile("woven0%d" % h, [P, HALF, PACK], BF16) for h in range(2)], [woven1[:, cols(h), :] for h in range(2)]]
         x_codes = [tile("x_codes%d" % i, [P, J], U32) for i in range(2)]
         x_sc = [tile("x_sc%d" % i, [P, J], U8) for i in range(2)]
         streams = ((idx2, gb_t), (idx1, ga_t))
@@ -115,38 +116,46 @@ def tile_list_scaledpartner_twosteps_store_plain_kernel(
             for h in range(2):
                 copy = nc.vector.tensor_copy if i == 0 else nc.scalar.copy
                 copy(woven[i][h][:, :, n_early[i] :], late[i][:, :, cols(h)].rearrange("p t j -> p j t"))
-            for h in range(2):
+            if i == 0:
+                for h in range(2):
+                    nc.vector.quantize_mx(
+                        out=x_codes[i][:, cols(h)].bitcast(E4M3),
+                        scales=x_sc[i][:, cols(h)],
+                        in_=woven[i][h][:].rearrange("p j t -> p (j t)"),
+                    )
+            else:
                 nc.vector.quantize_mx(
-                    out=x_codes[i][:, cols(h)].bitcast(E4M3),
-                    scales=x_sc[i][:, cols(h)],
-                    in_=woven[i][h][:].rearrange("p j t -> p (j t)"),
+                    out=x_codes[i][:].bitcast(E4M3), scales=x_sc[i][:], in_=woven1[:].rearrange("p j t -> p (j t)")
                 )
 
 
-        def first_stage(dst, t, i, h):
+        def first_stage(dst, t, i, slots):
             nc.tensor.matmul_mx(
                 dst,
                 lhsT=w_dealt[:, t, :].bitcast(E2M1),
                 lhsT_scale=w_sc[:, t, :],
-                rhs=x_codes[i][:, cols(h)].bitcast(E4M3),
-                rhs_scale=x_sc[i][:, cols(h)],
+                rhs=x_codes[i][:, slots].bitcast(E4M3),
+                rhs_scale=x_sc[i][:, slots],
                 start=True,
                 stop=True,
             )
 
-        b_ps = [psum.tile([P, J], F32, name="b_ps%d" % t, tag="b_ps%d" % t) for t in range(PACK)]
         b_sb = [tile("b_sb%d" % t, [P, J], F32) for t in range(PACK)]
-        for t in range(PACK):
-            for h in range(2):
-                first_stage(b_ps[t][:, cols(h)], t, 0, h)
-            if t == 0:
-                nc.scalar.copy(b_sb[t][:], b_ps[t][:])
+        for h in range(2):
+            b_half = psum.tile([P, HALF], F32, name="b_half%d" % h, tag="b_half%d" % h)
+            first_stage(b_half[:], 0, 0, cols(h))
+            nc.scalar.copy(b_sb[0][:, cols(h)], b_half[:])
+        for t in range(1, PACK):
+            b_ps = psum.tile([P, J], F32, name="b_ps%d" % t, tag="b_ps%d" % t)
+            first_stage(b_ps[:], t, 0, slice(0, J))
+            if t == 1:
+                nc.scalar.copy(b_sb[t][:], b_ps[:])
             else:
-                nc.vector.tensor_copy(b_sb[t][:], b_ps[t][:])
+                nc.vector.tensor_copy(b_sb[t][:], b_ps[:])
         a_ps = [psum.tile([P, PACK, HALF], F32, name="a_ps%d" % h) for h in range(2)]
         for h in range(2):
             for t in range(PACK):
-                first_stage(a_ps[h][:, t, :], t, 1, h)
+                first_stage(a_ps[h][:, t, :], t, 1, cols(h))
 
         vs_codes = tile("vs_codes", [P, N], U32, tag="woven01")
         nc.vector.tensor_copy(vs_codes[:], vs_table[:].bitcast(U32).indirect(idx4[:]))
@@ -157,9 +166,9 @@ def tile_list_scaledpartner_twosteps_store_plain_kernel(
         hid_sc = [tile("hid_sc%d" % h, [P, HALF], U8) for h in range(2)]
         for h in range(2):
             diff.append(tile("diff%d" % h, [P, PACK, HALF], F32, tag="diff"))
-            groups = [(t, t + 1) for t in range(PACK)] if h == 0 else [(0, PACK - 1), (PACK - 1, PACK)]
-            for lo, hi in groups:
-                partner = tile("partner%d%d" % (h, lo), [P, hi - lo, HALF], F32, tag="partner%d" % lo)
+            cut = 2 if h == 0 else 3
+            for g, (lo, hi) in enumerate(((0, cut), (cut, PACK))):
+                partner = tile("partner%d%d" % (h, lo), [P, hi - lo, HALF], F32, tag="partner%d" % g)
                 for t in range(lo, hi):
                     nc.scalar.activation(
                         partner[:, t - lo, :],
@@ -193,7 +202,7 @@ def tile_list_scaledpartner_twosteps_store_plain_kernel(
                 )
 
             if h == 0:
-                y_ps = psum.tile([P, 2, HALF], F32, name="y_ps0", tag="b_ps0")
+                y_ps = psum.tile([P, 2, HALF], F32, name="y_ps0", tag="b_ps3")
                 y_sb = tile("y_sb0", [P, 2, HALF], F32)
                 for u in range(2):
                     second_stage(y_ps[:, u, :], u)

from contextlib import ExitStack

import concourse.mybir as mybir

K, T, J, R, N, S = 512, 1024, 256, 512, 256, 1024
FLOPS = 2 * K * R * J * 2 + 2 * R * N * J

F32 = mybir.dt.float32
BF16 = mybir.dt.bfloat16
I32 = mybir.dt.int32
U32 = mybir.dt.uint32
U16 = mybir.dt.uint16
U8 = mybir.dt.uint8
E4M3 = mybir.dt.float8_e4m3fn_x4
E5M2 = mybir.dt.float8_e5m2_x4
E2M1 = mybir.dt.float4_e2m1fn_x4
ACT = mybir.ActivationFunctionType
ALU = mybir.AluOpType

P = 128
PACK = 4
HALF = J // 2
LIST_COLS = 16


def tile_list_scaledpartner_twosteps_store_plain_kernel(
    tc, cq, ga, gb, w_words, w_scales, sa, vs_words, vs_scales, offs, offs2, offs3, offs4, out
):
    nc = tc.nc
    with ExitStack() as ctx:
        lists = ctx.enter_context(tc.tile_pool(name="lists", bufs=1))
        sb = ctx.enter_context(tc.tile_pool(name="sb", bufs=1))
        psum = ctx.enter_context(tc.psum_pool(name="psum", bufs=1))

        def tile(name, shape, dtype, tag=None):
            return sb.tile(shape, dtype, name=name, tag=tag or name, align_bytes=64)

        def list_tile(name):
            return lists.tile([P, LIST_COLS], U16, name=name)

        idx1, idx2, idx3, idx4 = [list_tile("idx%d" % i) for i in range(1, 5)]
        cq_rows = cq.rearrange("(p t) c -> p t c", t=PACK)
        table = [tile("table%d" % t, [P, T], F32) for t in range(PACK)]
        ga_t, gb_t, sa_t = [tile(n, [P, PACK], F32) for n in ("ga_t", "gb_t", "sa_t")]
        w_raw = tile("w_raw", [P, R], U16)
        ws_rows = tile("ws_rows", [PACK, PACK, R // 4], I32)
        vss_rows = [tile("vss_rows%d" % g, [P, 2, S // 4], I32) for g in range(2)]
        vs_table = tile("vs_table", [P, S], I32)

        def by_partition(v):
            return v.rearrange("(p t) o -> p (t o)", t=PACK)

        def scale_rows(v):
            return v[0].bitcast(I32).rearrange("(q r) c -> r q c", r=PACK)

        nc.sync.dma_start(vss_rows[0][0:PACK, :, :], scale_rows(vs_scales)[:, 0:2, :])
        nc.scalar.dma_start(vss_rows[1][64 : 64 + PACK, :, :], scale_rows(vs_scales)[:, 2:4, :])
        nc.sync.dma_start(idx2[:], offs2)
        nc.sync.dma_start(table[0][:], cq_rows[:, 0, :])
        nc.scalar.dma_start(gb_t[:], by_partition(gb))
        nc.sync.dma_start(idx1[:], offs)
        nc.scalar.dma_start(ga_t[:], by_partition(ga))
        nc.sync.dma_start(table[1][:], cq_rows[:, 1, :])
        nc.sync.dma_start(ws_rows[:], scale_rows(w_scales))
        nc.sync.dma_start(w_raw[:].bitcast(I32), w_words[0].bitcast(I32))
        nc.sync.dma_start(table[2][:], cq_rows[:, 2, :])
        nc.sync.dma_start(idx4[:], offs4)
        nc.sync.dma_start(table[3][:], cq_rows[:, 3, :])
        nc.sync.dma_start(vs_table[:], vs_words[0].rearrange("p n t -> p (n t)").bitcast(I32))
        nc.sync.dma_start(idx3[:], offs3)
        nc.sync.dma_start(sa_t[:], by_partition(sa))

        warm = tile("warm", [P, 8], F32)
        nc.vector.memset(warm[:, 0:1], 0.0)
        nc.scalar.activation(warm[:, 1:2], warm[:, 0:1], ACT.Copy)

        def spread(name, rows, width):
            plane = tile(name, [P, width], U8)
            nc.vector.memset(plane[:].bitcast(I32), 0)
            for q in range(PACK):
                nc.vector.tensor_copy(plane[32 * q : 32 * q + PACK, :].bitcast(I32), rows[q])
            return plane

        vss_plane = spread("vss_plane", [vss_rows[q // 2][64 * (q // 2) : 64 * (q // 2) + PACK, q % 2, :] for q in range(PACK)], S)
        ws_plane = spread("ws_plane", [ws_rows[:, q, :] for q in range(PACK)], R)
        w_sc = tile("w_sc", [P, PACK, P], U8)
        nc.vector.tensor_copy(w_sc[:], ws_plane[:].rearrange("p (m t) -> p t m", t=PACK))
        w_dealt = tile("w_dealt", [P, PACK, P], U16)
        nc.vector.tensor_copy(w_dealt[:], w_raw[:].rearrange("p (m t) -> p t m", t=PACK))
        vs_sc = tile("vs_sc", [P, N], U8)
        nc.vector.tensor_copy(vs_sc[:], vss_plane[:].indirect(idx4[:]))

        def cols(h):
            return slice(h * HALF, (h + 1) * HALF)

        n_early = (3, 2)
        early = [tile("early%d" % i, [P, n_early[i], J], BF16) for i in range(2)]
        late = [tile("late0", [P, 1, J], BF16), tile("late1", [P, 2, J], BF16)]
        woven1 = tile("woven1", [P, J, PACK], BF16)
        woven = [[tile("woven0%d" % h, [P, HALF, PACK], BF16) for h in range(2)], [woven1[:, cols(h), :] for h in range(2)]]
        x_codes = [tile("x_codes%d" % i, [P, J], U32) for i in range(2)]
        x_sc = [tile("x_sc%d" % i, [P, J], U8) for i in range(2)]
        streams = ((idx2, gb_t), (idx1, ga_t))

        for t in range(PACK):
            for i, (idx, step) in enumerate(streams):
                dst = early[i][:, t, :] if t < n_early[i] else late[i][:, t - n_early[i], :]
                nc.scalar.activation(dst, table[t][:].indirect(idx[:]), ACT.Copy, scale=step[:, t : t + 1])
                if t == n_early[i] - 1:
                    for h in range(2):
                        nc.vector.tensor_copy(
                            woven[i][h][:, :, : n_early[i]], early[i][:, :, cols(h)].rearrange("p t j -> p j t")
                        )

        for i in range(2):
            for h in range(2):
                copy = nc.vector.tensor_copy if i == 0 else nc.scalar.copy
                copy(woven[i][h][:, :, n_early[i] :], late[i][:, :, cols(h)].rearrange("p t j -> p j t"))
            if i == 0:
                for h in range(2):
                    nc.vector.quantize_mx(
                        out=x_codes[i][:, cols(h)].bitcast(E4M3),
                        scales=x_sc[i][:, cols(h)],
                        in_=woven[i][h][:].rearrange("p j t -> p (j t)"),
                    )
            else:
                nc.vector.quantize_mx(
                    out=x_codes[i][:].bitcast(E4M3), scales=x_sc[i][:], in_=woven1[:].rearrange("p j t -> p (j t)")
                )


        def first_stage(dst, t, i, slots):
            nc.tensor.matmul_mx(
                dst,
                lhsT=w_dealt[:, t, :].bitcast(E2M1),
                lhsT_scale=w_sc[:, t, :],
                rhs=x_codes[i][:, slots].bitcast(E4M3),
                rhs_scale=x_sc[i][:, slots],
                start=True,
                stop=True,
            )

        b_sb = [tile("b_sb%d" % t, [P, J], F32) for t in range(PACK)]
        for h in range(2):
            b_half = psum.tile([P, HALF], F32, name="b_half%d" % h, tag="b_half%d" % h)
            first_stage(b_half[:], 0, 0, cols(h))
            nc.scalar.copy(b_sb[0][:, cols(h)], b_half[:])
        for t in range(1, PACK):
            b_ps = psum.tile([P, J], F32, name="b_ps%d" % t, tag="b_ps%d" % t)
            first_stage(b_ps[:], t, 0, slice(0, J))
            if t == 1:
                nc.scalar.copy(b_sb[t][:], b_ps[:])
            else:
                nc.vector.tensor_copy(b_sb[t][:], b_ps[:])
        a_ps = [psum.tile([P, PACK, HALF], F32, name="a_ps%d" % h) for h in range(2)]
        for h in range(2):
            for t in range(PACK):
                first_stage(a_ps[h][:, t, :], t, 1, cols(h))

        vs_codes = tile("vs_codes", [P, N], U32, tag="woven01")
        nc.vector.tensor_copy(vs_codes[:], vs_table[:].bitcast(U32).indirect(idx4[:]))

        diff = []
        hid = [tile("hid%d" % h, [P, HALF, PACK], BF16) for h in range(2)]
        hid_codes = [tile("hid_codes%d" % h, [P, HALF], U32) for h in range(2)]
        hid_sc = [tile("hid_sc%d" % h, [P, HALF], U8) for h in range(2)]
        for h in range(2):
            diff.append(tile("diff%d" % h, [P, PACK, HALF], F32, tag="diff"))
            cut = 2 if h == 0 else 3
            for g, (lo, hi) in enumerate(((0, cut), (cut, PACK))):
                partner = tile("partner%d%d" % (h, lo), [P, hi - lo, HALF], F32, tag="partner%d" % g)
                for t in range(lo, hi):
                    nc.scalar.activation(
                        partner[:, t - lo, :],
                        b_sb[t][:].indirect(idx3[:, h * 8 : (h + 1) * 8]),
                        ACT.Copy,
                        scale=sa_t[:, t : t + 1],
                    )
                nc.vector.tensor_tensor(diff[h][:, lo:hi, :], a_ps[h][:, lo:hi, :], partner[:], ALU.subtract)
            on_vector = HALF if h == 0 else 48
            by_slot = diff[h][:, :, :on_vector].rearrange("p t j -> p j t")
            nc.vector.scalar_tensor_tensor(hid[h][:, :on_vector, :], by_slot, -1.0, by_slot, ALU.mult, ALU.max)
            if on_vector < HALF:
                nc.scalar.activation(
                    hid[h][:, on_vector:, :].rearrange("p (c i) t -> p c t i", i=4),
                    diff[h][:, :, on_vector:].rearrange("p t (c i) -> p c t i", i=4),
                    ACT.Abs,
                )
        out_rows = out.rearrange("(u p) j -> p u j", p=P)
        for h in range(2):
            nc.vector.quantize_mx(out=hid_codes[h][:].bitcast(E4M3), scales=hid_sc[h][:], in_=hid[h][:].rearrange("p j t -> p (j t)"))

            def second_stage(dst, u):
                nc.tensor.matmul_mx(
                    dst,
                    lhsT=vs_codes[:, u * P : (u + 1) * P].bitcast(E5M2),
                    lhsT_scale=vs_sc[:, u * P : (u + 1) * P],
                    rhs=hid_codes[h][:].bitcast(E4M3),
                    rhs_scale=hid_sc[h][:],
                    start=True,
                    stop=True,
                )

            if h == 0:
                y_ps = psum.tile([P, 2, HALF], F32, name="y_ps0", tag="b_ps3")
                y_sb = tile("y_sb0", [P, 2, HALF], F32)
                for u in range(2):
                    second_stage(y_ps[:, u, :], u)
                nc.scalar.copy(y_sb[:], y_ps[:])
                nc.sync.dma_start(out_rows[:, :, cols(h)], y_sb[:])
            else:
                for u in range(2):
                    y_ps = psum.tile([P, HALF], F32, name="y_ps1%d" % u, tag="b_ps%d" % (1 + u))
                    y_sb = tile("y_sb1%d" % u, [P, HALF], F32)
                    second_stage(y_ps[:], u)
                    if u == 0:
                        nc.vector.tensor_copy(y_sb[:], y_ps[:])
                        nc.sync.dma_start(out_rows[:, u, cols(h)], y_sb[:])
                    else:
                        nc.scalar.copy(y_sb[:], y_ps[:])
                        nc.scalar.dma_start(out_rows[:, u, cols(h)], y_sb[:])
